import numpy as np
import ml_dtypes


def mxq(x, axis, fmt="e4m3"):
    dtype, down = {"e4m3": (ml_dtypes.float8_e4m3fn, 7), "e5m2": (ml_dtypes.float8_e5m2, 14)}[fmt]
    v = np.moveaxis(np.asarray(x, np.float32).astype(ml_dtypes.bfloat16).astype(np.float64), axis, -1)
    blocks = v.reshape(v.shape[:-1] + (-1, 32))
    amax = np.abs(blocks).max(-1, keepdims=True)
    byte = np.maximum(np.where(amax > 0, np.frexp(amax)[1] - 1 + 127, 0) - down, 1)
    scale = np.exp2(byte - 127.0)
    codes = (blocks / scale).astype(np.float32).astype(dtype).astype(np.float64)
    return np.moveaxis((codes * scale).reshape(v.shape), -1, axis)


WIDE = False


def mx_kscale(k):
    if not WIDE:
        return np.ones(k)
    levels = np.array([10, -10, 5, -5, 0])
    if k % 512:
        return np.exp2(np.random.permutation(np.resize(levels, k // 32))).repeat(32)
    a = np.empty((k // 512, 16))
    for p in range(k // 512):
        a[p, :8] = np.random.permutation(np.resize(levels, 8))
        for g in range(8):
            far = levels[np.abs(levels - a[p, g]) >= 10]
            a[p, g + 8] = far[np.random.randint(len(far))]
    return np.exp2(a.ravel()).repeat(32)


BF16 = ml_dtypes.bfloat16


def bf(x):
    return np.asarray(x, np.float32).astype(BF16)


def f64(x):
    return np.asarray(x).astype(np.float64)


E2M1 = np.array([0.0, 0.5, 1.0, 1.5, 2.0, 3.0, 4.0, 6.0, -0.0, -0.5, -1.0, -1.5, -2.0, -3.0, -4.0, -6.0])


def pack_weight(w, fmt):
    k, n = w.shape
    w = f64(bf(w)).reshape(k // 32, 32, n)
    amax = np.abs(w).max(1)
    if fmt == "e4m3":
        byte = np.frexp(amax)[1] - 1 + 127 - 7
    else:
        mant, ex = np.frexp(amax / 6.0)
        byte = np.where(mant > 0.5, ex, ex - 1) + 127
    byte = np.clip(np.where(amax > 0, byte, 1), 1, 254)
    scaled = (w * np.exp2(127.0 - byte)[:, None, :]).reshape(k, n).astype(np.float32)
    by_word = np.ascontiguousarray(scaled.reshape(k // 512, 128, 4, n).transpose(0, 1, 3, 2))
    if fmt == "e4m3":
        words = by_word.astype(ml_dtypes.float8_e4m3fn).view(np.uint8)
    else:
        c = by_word.astype(ml_dtypes.float4_e2m1fn).view(np.uint8) & 0xF
        words = c[..., 0::2] | (c[..., 1::2] << 4)
    return np.ascontiguousarray(words), np.ascontiguousarray(byte.astype(np.uint8).reshape(k // 512, 16, n))


def unpack_weight(words, scales, fmt):
    g, p, n, _ = words.shape
    if fmt == "e4m3":
        vals = np.ascontiguousarray(words).view(ml_dtypes.float8_e4m3fn).astype(np.float64)
    else:
        nib = np.empty((g, p, n, 4), np.uint8)
        nib[..., 0::2] = words & 0xF
        nib[..., 1::2] = words >> 4
        vals = E2M1[nib]
    vals = vals * np.repeat(np.exp2(scales.astype(np.float64) - 127.0), 8, axis=1)[..., None]
    return vals.transpose(0, 1, 3, 2).reshape(g * 512, n)
def pack4(w):
    words, scales = pack_weight(w, "e2m1")
    return words.reshape(words.shape[0], 128, -1), scales


def unpack4(words, scales):
    return unpack_weight(words.reshape(words.shape[0], 128, -1, 2), scales, "e2m1")


def planes(Y):
    n, m = Y.shape
    b = f64(bf(Y)).reshape(n // 32, 32, m)
    amax = np.abs(b).max(1)
    byte = np.clip(np.where(amax > 0, np.frexp(amax)[1] - 1 + 127 - 7, 1), 1, 254)
    codes = (b * np.exp2(127.0 - byte)[:, None, :]).reshape(n, m).astype(np.float32).astype(ml_dtypes.float8_e4m3fn).view(np.uint8)
    words = codes.reshape(n // 512, 128, 4, m).transpose(0, 1, 3, 2)
    return np.ascontiguousarray(words), np.ascontiguousarray(byte.astype(np.uint8).reshape(n // 512, 16, m))


J, K, N = 1024, 1536, 512

SHIFT_SLOW, SHIFT_MID, SHIFT_FAST = 0.4, 1.0, 2.0

def observed_resolvent(A, C, shift):
    return np.linalg.solve(shift * np.eye(len(A)) - A.T, C.T)

def setup_inputs():
    s = mx_kscale(K)
    A = 0.9 * np.random.randn(K, K) / np.sqrt(K) - np.eye(K)
    C = np.random.randn(N, K) / np.sqrt(K)
    X = np.random.randn(K, J) * np.exp(0.8 * np.random.randn(J))
    x_words, x_scales = pack_weight(X * s[:, None], "e4m3")
    w_slow = bf(observed_resolvent(A, C, SHIFT_SLOW) / s[:, None])
    mid_words, mid_scales = pack_weight(observed_resolvent(A, C, SHIFT_MID) / s[:, None], "e4m3")
    fast_words, fast_scales = pack4(observed_resolvent(A, C, SHIFT_FAST) / s[:, None])
    c_slow = bf(np.exp(0.3 * np.random.randn(N)))
    c_mid = bf(np.exp(0.3 * np.random.randn(N)))
    return {"x_words": x_words, "x_scales": x_scales, "w_slow": w_slow,
            "mid_words": mid_words, "mid_scales": mid_scales,
            "fast_words": fast_words, "fast_scales": fast_scales,
            "c_slow": c_slow, "c_mid": c_mid}

def reference(x_words, x_scales, w_slow, mid_words, mid_scales, fast_words, fast_scales, c_slow, c_mid):
    X = unpack_weight(x_words, x_scales, "e4m3")
    W_mid = unpack_weight(mid_words, mid_scales, "e4m3")
    W_fast = unpack4(fast_words, fast_scales)
    W_slow = mxq(f64(w_slow), 0, "e4m3")
    slow = X.T @ W_slow
    mid = X.T @ W_mid
    fast = X.T @ W_fast
    y = f64(c_slow) * slow + f64(c_mid) * mid + fast
    Y = y.reshape(J, N)
    words, scales = planes(Y)
    return y, words, scales

@@ -1,0 +1,282 @@
+from contextlib import ExitStack
+
+import concourse.mybir as mybir
+from concourse.masks import make_identity
+
+J, K, N = 1024, 1536, 512
+FLOPS = 3 * 2 * J * K * N
+
+F32 = mybir.dt.float32
+BF16 = mybir.dt.bfloat16
+I32 = mybir.dt.int32
+U8 = mybir.dt.uint8
+FP8X4 = mybir.dt.float8_e4m3fn_x4
+FP4X4 = mybir.dt.float4_e2m1fn_x4
+MULT = mybir.AluOpType.mult
+ADD = mybir.AluOpType.add
+
+P = 128
+PACK = 4
+GROUP = P * PACK
+PASSES = K // GROUP
+TILES = N // P
+WARM = 4
+
+
+def tile_windowed_resolvent_response_k3_kernel(
+    tc, x_words, x_scales, w_slow, mid_words, mid_scales, fast_words, fast_scales, c_slow, c_mid, out_0, out_1, out_2
+):
+    nc = tc.nc
+    with ExitStack() as ctx:
+        sb = ctx.enter_context(tc.tile_pool(name="sb", bufs=1))
+        ps = ctx.enter_context(tc.psum_pool(name="ps", bufs=1))
+        ctx.enter_context(tc.manual_schedule())
+
+        def sbuf(name, shape, dtype):
+            return sb.tile(shape, dtype, name=name, align_bytes=64)
+
+        bank = [ps.tile([P, N], F32, name="bank%d" % b) for b in range(8)]
+
+        c_rows = sbuf("c_rows", [P, P], BF16)
+        ident_bf = sbuf("ident_bf", [P, P], BF16)
+        ident_f32 = sbuf("ident_f32", [P, P], F32)
+        warm = sbuf("warm", [P, N], BF16)
+        c_cols = sbuf("c_cols", [P, 2 * TILES], F32)
+        cs_wide = sbuf("cs_wide", [P, N], F32)
+        cm_wide = sbuf("cm_wide", [P, N], F32)
+        xs = sbuf("xs", [P, PASSES, J], U8)
+        fs = sbuf("fs", [P, PASSES, N], U8)
+        ms = sbuf("ms", [P, PASSES, N], U8)
+        xw = [[sbuf("xw%d_%d" % (h, g), [P, GROUP], I32) for g in range(PASSES)] for h in range(2)]
+        xp = [sbuf("xp%d" % g, [P, PACK, P], I32) for g in range(PASSES)]
+        xps = [sbuf("xps%d" % g, [P, PACK, P], U8) for g in range(PASSES)]
+        fw = sbuf("fw", [P, PASSES, 2 * N], U8)
+        mw = sbuf("mw", [P, PASSES, N], I32)
+        w_raw = [sbuf("w_raw%d" % g, [P, PACK, N], BF16) for g in range(PASSES)]
+        w_grp = [sbuf("w_grp%d" % g, [P, N * PACK], BF16) for g in range(PASSES)]
+        sw = [sbuf("sw%d" % g, [P, N], I32) for g in range(PASSES)]
+        ss = [sbuf("ss%d" % g, [P, N], U8) for g in range(PASSES)]
+        f_t = [sbuf("f_t%d" % a, [P, PACK, P], F32) for a in range(TILES)]
+        p_t = [sbuf("p_t%d" % a, [P, PACK, P], F32) for a in range(TILES)]
+        y_t = [sbuf("y_t%d" % a, [P, PACK, P], F32) for a in range(TILES)]
+        m_n = [sbuf("m_n%d" % t, [P, N], F32) for t in range(PACK)]
+        s_n = [sbuf("s_n%d" % t, [P, N], F32) for t in range(PACK)]
+        q_n = sbuf("q_n", [P, PACK, N], F32)
+        y32 = [[sbuf("y32_%d_%d" % (h, a), [P, PACK, P], F32) for a in range(TILES)] for h in range(2)]
+        y16 = [[sbuf("y16_%d_%d" % (h, a), [P, P * PACK], BF16) for a in range(TILES)] for h in range(2)]
+        yq = [sbuf("yq%d" % h, [P, N], I32) for h in range(2)]
+        ysc = sbuf("ysc", [P, 2, N], U8)
+
+        def cols(a, n=1):
+            return slice(a * P, (a + n) * P)
+
+        def load_scales(eng, plane, src):
+            for r in range(4):
+                eng.dma_start(
+                    out=plane[r:P:32, :, :].bitcast(I32),
+                    in_=src[:, r:16:4, :].rearrange("g q n -> q g n").bitcast(I32),
+                )
+
+        def load_x(h, g):
+            src = x_words[g].rearrange("p n t -> p (n t)").bitcast(I32)
+            nc.sync.dma_start(out=xw[h][g][:], in_=src[:, h * GROUP : (h + 1) * GROUP])
+
+        def load_w(g):
+            nc.sync.dma_start(
+                out=w_raw[g][:], in_=w_slow[g * GROUP : (g + 1) * GROUP, :].rearrange("(p t) n -> p t n", t=PACK)
+            )
+
+        def group_w(copy, g, a, n):
+            copy(
+                out=w_grp[g][:, a * GROUP : (a + n) * GROUP].rearrange("p (c i t) -> p c t i", i=4, t=PACK),
+                in_=w_raw[g][:, :, cols(a, n)].rearrange("p t (c i) -> p c t i", i=4),
+            )
+
+        def quant_w(g, a, n):
+            nc.vector.quantize_mx(
+                out=sw[g][:, cols(a, n)].bitcast(FP8X4),
+                scales=ss[g][:, cols(a, n)],
+                in_=w_grp[g][:, a * GROUP : (a + n) * GROUP],
+            )
+
+        def weight(kind, g, a, n):
+            if kind == "slow":
+                return sw[g][:, cols(a, n)].bitcast(FP8X4), ss[g][:, cols(a, n)]
+            if kind == "mid":
+                return mw[:, g, cols(a, n)].bitcast(FP8X4), ms[:, g, cols(a, n)]
+            return fw[:, g, 2 * a * P : 2 * (a + n) * P].bitcast(FP4X4), fs[:, g, cols(a, n)]
+
+        def pass_sensors(kind, g, a, b):
+            w, s = weight(kind, g, a, 1)
+            nc.tensor.matmul_mx(
+                out=bank[b][:], lhsT=w, lhsT_scale=s, rhs=xw[0][g][:].bitcast(FP8X4), rhs_scale=xs[:, g, 0:GROUP],
+                start=(g == 0), stop=(g == PASSES - 1),
+            )
+
+        def pass_modes(kind, g, t, out, a, n):
+            w, s = weight(kind, g, a, n)
+            nc.tensor.matmul_mx(
+                out=out, lhsT=xp[g][:, t, :].bitcast(FP8X4), lhsT_scale=xps[g][:, t, :], rhs=w, rhs_scale=s,
+                start=(g == 0), stop=(g == PASSES - 1),
+            )
+
+        def sorted_bank(b):
+            return bank[b][:].rearrange("i (m t) -> i t m", t=PACK)
+
+        def sort_x(g):
+            nc.vector.tensor_copy(
+                out=xp[g][:].rearrange("p t (c i) -> p c t i", i=4),
+                in_=xw[1][g][:].rearrange("p (c i t) -> p c t i", i=4, t=PACK),
+            )
+            nc.vector.tensor_copy(
+                out=xps[g][:].rearrange("p t (c i) -> p c t i", i=16),
+                in_=xs[:, g, GROUP:J].rearrange("p (c i t) -> p c t i", i=16, t=PACK),
+            )
+
+        def turn(a, b):
+            for t in range(PACK):
+                nc.tensor.transpose(bank[b][:, cols(t)], y_t[a][:, t, :], ident_f32[:])
+
+        def quant_y(h, a):
+            nc.vector.quantize_mx(
+                out=yq[h][:, cols(a)].bitcast(FP8X4), scales=ysc[:, h, cols(a)], in_=y16[h][a][:]
+            )
+
+        def store_y(h, a):
+            rows = out_0[h * GROUP : (h + 1) * GROUP, cols(a)]
+            nc.sync.dma_start(out=rows.rearrange("(p t) m -> p t m", t=PACK), in_=y32[h][a][:])
+
+        def store_words(h, a, n):
+            dst = out_1[h].rearrange("p n t -> p (n t)").bitcast(I32)
+            nc.sync.dma_start(out=dst[:, cols(a, n)], in_=yq[h][:, cols(a, n)])
+
+        nc.vector.memset(c_rows[:], 0.0)
+        nc.vector.memset(xs[:].bitcast(I32), 0)
+        nc.vector.memset(fs[:].bitcast(I32), 0)
+        nc.vector.memset(ms[:].bitcast(I32), 0)
+        nc.gpsimd.memset(warm[:], 0.0)
+        make_identity(nc, ident_bf[:])
+        make_identity(nc, ident_f32[:])
+        nc.scalar.dma_start(out=c_rows[0:TILES, :], in_=c_slow.rearrange("(a p) -> a p", p=P))
+        nc.scalar.dma_start(out=c_rows[TILES : 2 * TILES, :], in_=c_mid.rearrange("(a p) -> a p", p=P))
+        load_scales(nc.scalar, xs, x_scales)
+        load_w(0)
+        load_x(0, 0)
+        load_scales(nc.sync, fs, fast_scales)
+        nc.sync.dma_start(out=fw[:].bitcast(I32), in_=fast_words.rearrange("g p n -> p g n").bitcast(I32))
+        load_x(0, 1)
+        load_w(1)
+        load_x(0, 2)
+        load_w(2)
+        load_scales(nc.sync, ms, mid_scales)
+        nc.sync.dma_start(out=mw[:], in_=mid_words.rearrange("g p n t -> p g (n t)").bitcast(I32))
+        for g in range(PASSES):
+            load_x(1, g)
+
+        for w in range(WARM):
+            nc.tensor.matmul(bank[4][:], lhsT=warm[:, 0:P], rhs=warm[:], start=True, stop=True)
+        nc.tensor.matmul(bank[5][:, 0 : 2 * TILES], lhsT=c_rows[:], rhs=ident_bf[:, 0 : 2 * TILES], start=True, stop=True)
+        for row in range(2 * TILES):
+            nc.tensor.matmul(
+                bank[6 + row // TILES][:, cols(row % TILES)],
+                lhsT=ident_bf[:, row : row + 1].to_broadcast([P, P]), rhs=c_rows[:], start=True, stop=True,
+            )
+
+        group_w(nc.vector.tensor_copy, 0, 0, 1)
+        group_w(nc.scalar.copy, 0, 1, 1)
+        group_w(nc.vector.tensor_copy, 0, 2, 1)
+        group_w(nc.scalar.copy, 0, 3, 1)
+        quant_w(0, 0, 1)
+        quant_w(0, 1, 1)
+        quant_w(0, 2, 1)
+        nc.vector.tensor_copy(out=c_cols[:], in_=bank[5][:, 0 : 2 * TILES])
+        quant_w(0, 3, 1)
+        nc.scalar.copy(out=cs_wide[:], in_=bank[6][:])
+        nc.scalar.copy(out=cm_wide[:], in_=bank[7][:])
+
+        for a in range(TILES):
+            pass_sensors("slow", 0, a, a)
+        for g in (0, 1):
+            for a in range(TILES):
+                pass_sensors("fast", g, a, 4 + a)
+        for g in (1, 2):
+            group_w(nc.vector.tensor_copy, g, 0, 2)
+            group_w(nc.scalar.copy, g, 2, 2)
+            quant_w(g, 0, 2)
+            quant_w(g, 2, 2)
+        for a in range(TILES):
+            pass_sensors("slow", 1, a, a)
+        for a in range(TILES):
+            pass_sensors("fast", 2, a, 4 + a)
+            nc.scalar.copy(out=f_t[a][:], in_=sorted_bank(4 + a))
+        for a in range(TILES):
+            pass_sensors("slow", 2, a, a)
+            nc.vector.scalar_tensor_tensor(
+                out=p_t[a][:], in0=sorted_bank(a), scalar=c_cols[:, a : a + 1], in1=f_t[a][:], op0=MULT, op1=ADD
+            )
+        for a in range(TILES):
+            for g in range(PASSES):
+                pass_sensors("mid", g, a, 4 + a)
+            if a < PASSES:
+                sort_x(a)
+            nc.vector.scalar_tensor_tensor(
+                out=y_t[a][:], in0=sorted_bank(4 + a), scalar=c_cols[:, TILES + a : TILES + a + 1], in1=p_t[a][:],
+                op0=MULT, op1=ADD,
+            )
+
+        def leave_turned(a, b):
+            nc.scalar.copy(
+                out=y16[0][a][:].rearrange("p (i t) -> p i t", t=PACK),
+                in_=bank[b][:].rearrange("p (t i) -> p i t", t=PACK),
+            )
+            nc.scalar.copy(out=y32[0][a][:], in_=bank[b][:].rearrange("p (t i) -> p t i", t=PACK))
+            store_y(0, a)
+
+        def mid_and_slow(t, b):
+            for g in range(PASSES):
+                pass_modes("mid", g, t, bank[b][:], 0, TILES)
+            nc.vector.tensor_tensor(out=m_n[t][:], in0=bank[b][:], in1=cm_wide[:], op=MULT)
+            for g in range(PASSES):
+                pass_modes("slow", g, t, bank[b + 1][:], 0, TILES)
+            nc.vector.tensor_tensor(out=s_n[t][:], in0=bank[b + 1][:], in1=cs_wide[:], op=MULT)
+            adder = nc.vector if t == PACK - 1 else nc.gpsimd
+            adder.tensor_tensor(out=q_n[:, t, :], in0=m_n[t][:], in1=s_n[t][:], op=ADD)
+
+        for a in (0, 1):
+            turn(a, a)
+            leave_turned(a, a)
+        mid_and_slow(0, 2)
+        quant_y(0, 0)
+        for a in (2, 3):
+            turn(a, 2 + a)
+            leave_turned(a, 2 + a)
+        mid_and_slow(1, 6)
+        quant_y(0, 1)
+        quant_y(0, 2)
+        mid_and_slow(2, 0)
+        quant_y(0, 3)
+        store_words(0, 0, TILES)
+        mid_and_slow(3, 2)
+
+        for a in range(TILES):
+            for t in range(PACK):
+                for g in range(PASSES):
+                    pass_modes("fast", g, t, bank[4 + a][:, cols(t)], a, 1)
+            nc.vector.tensor_tensor(
+                out=y32[1][a][:], in0=bank[4 + a][:].rearrange("p (t i) -> p t i", t=PACK), in1=q_n[:, :, cols(a)], op=ADD
+            )
+            store_y(1, a)
+            nc.scalar.copy(
+                out=y16[1][a][:].rearrange("p (c i t) -> p c t i", i=4, t=PACK),
+                in_=y32[1][a][:].rearrange("p t (c i) -> p c t i", i=4),
+            )
+            if a > 0:
+                quant_y(1, a - 1)
+                store_words(1, a - 1, 1)
+        quant_y(1, TILES - 1)
+        store_words(1, TILES - 1, 1)
+        for r in range(4):
+            eng = nc.scalar if r % 2 else nc.sync
+            eng.dma_start(
+                out=out_2[:, r:16:4, :].rearrange("g q n -> q g n").bitcast(I32), in_=ysc[r:P:32, :, :].bitcast(I32)
+            )

@@ -20,7 +20,8 @@ PACK = 4
 GROUP = P * PACK
 PASSES = K // GROUP
 TILES = N // P
-WARM = 4
+WARM = 3
+BRIDGE = 3
 
 
 def tile_windowed_resolvent_response_k3_kernel(
@@ -44,7 +45,7 @@ def tile_windowed_resolvent_response_k3_kernel(
         c_cols = sbuf("c_cols", [P, 2 * TILES], F32)
         cs_wide = sbuf("cs_wide", [P, N], F32)
         cm_wide = sbuf("cm_wide", [P, N], F32)
-        xs = sbuf("xs", [P, PASSES, J], U8)
+        xs = [sbuf("xs%d" % h, [P, PASSES, GROUP], U8) for h in range(2)]
         fs = sbuf("fs", [P, PASSES, N], U8)
         ms = sbuf("ms", [P, PASSES, N], U8)
         xw = [[sbuf("xw%d_%d" % (h, g), [P, GROUP], I32) for g in range(PASSES)] for h in range(2)]
@@ -62,6 +63,7 @@ def tile_windowed_resolvent_response_k3_kernel(
         m_n = [sbuf("m_n%d" % t, [P, N], F32) for t in range(PACK)]
         s_n = [sbuf("s_n%d" % t, [P, N], F32) for t in range(PACK)]
         q_n = sbuf("q_n", [P, PACK, N], F32)
+        y_n = sbuf("y_n", [P, PACK, N], F32)
         y32 = [[sbuf("y32_%d_%d" % (h, a), [P, PACK, P], F32) for a in range(TILES)] for h in range(2)]
         y16 = [[sbuf("y16_%d_%d" % (h, a), [P, P * PACK], BF16) for a in range(TILES)] for h in range(2)]
         yq = [sbuf("yq%d" % h, [P, N], I32) for h in range(2)]
@@ -106,10 +108,10 @@ def tile_windowed_resolvent_response_k3_kernel(
                 return mw[:, g, cols(a, n)].bitcast(FP8X4), ms[:, g, cols(a, n)]
             return fw[:, g, 2 * a * P : 2 * (a + n) * P].bitcast(FP4X4), fs[:, g, cols(a, n)]
 
-        def pass_sensors(kind, g, a, b):
+        def pass_sensors(kind, g, a, b, h=0):
             w, s = weight(kind, g, a, 1)
             nc.tensor.matmul_mx(
-                out=bank[b][:], lhsT=w, lhsT_scale=s, rhs=xw[0][g][:].bitcast(FP8X4), rhs_scale=xs[:, g, 0:GROUP],
+                out=bank[b][:], lhsT=w, lhsT_scale=s, rhs=xw[h][g][:].bitcast(FP8X4), rhs_scale=xs[h][:, g, :],
                 start=(g == 0), stop=(g == PASSES - 1),
             )
 
@@ -130,7 +132,7 @@ def tile_windowed_resolvent_response_k3_kernel(
             )
             nc.vector.tensor_copy(
                 out=xps[g][:].rearrange("p t (c i) -> p c t i", i=16),
-                in_=xs[:, g, GROUP:J].rearrange("p (c i t) -> p c t i", i=16, t=PACK),
+                in_=xs[1][:, g, :].rearrange("p (c i t) -> p c t i", i=16, t=PACK),
             )
 
         def turn(a, b):
@@ -150,26 +152,58 @@ def tile_windowed_resolvent_response_k3_kernel(
             dst = out_1[h].rearrange("p n t -> p (n t)").bitcast(I32)
             nc.sync.dma_start(out=dst[:, cols(a, n)], in_=yq[h][:, cols(a, n)])
 
+
+        def load_f(g):
+            nc.sync.dma_start(out=fw[g][:].bitcast(I32), in_=fast_words[g].bitcast(I32))
+
+        def load_m(a, n):
+            src = mid_words.rearrange("g p n t -> p g (n t)").bitcast(I32)
+            nc.sync.dma_start(out=mw[:, :, cols(a, n)], in_=src[:, :, cols(a, n)])
+
+        def combine(out, b, col, other):
+            nc.vector.scalar_tensor_tensor(
+                out=out[:], in0=sorted_bank(b), scalar=c_cols[:, col : col + 1], in1=other[:], op0=MULT, op1=ADD
+            )
+
+        def leave_turned(h, a, b):
+            nc.scalar.copy(out=y32[h][a][:], in_=bank[b][:].rearrange("p (t i) -> p t i", t=PACK))
+            store_y(h, a)
+            nc.scalar.copy(
+                out=y16[h][a][:].rearrange("p (i t) -> p i t", t=PACK),
+                in_=bank[b][:].rearrange("p (t i) -> p i t", t=PACK),
+            )
+
+        def store_scales():
+            for r in range(4):
+                eng = nc.scalar if r % 2 else nc.sync
+                eng.dma_start(
+                    out=out_2[:, r:16:4, :].rearrange("g q n -> q g n").bitcast(I32), in_=ysc[r:P:32, :, :].bitcast(I32)
+                )
+
         nc.vector.memset(c_rows[:], 0.0)
-        nc.vector.memset(xs[:].bitcast(I32), 0)
+        nc.vector.memset(xs[0][:].bitcast(I32), 0)
+        nc.vector.memset(ident_bf[:], 0.0)
         nc.vector.memset(fs[:].bitcast(I32), 0)
         nc.vector.memset(ms[:].bitcast(I32), 0)
+        nc.vector.memset(xs[1][:].bitcast(I32), 0)
         nc.gpsimd.memset(warm[:], 0.0)
-        make_identity(nc, ident_bf[:])
+        make_identity(nc, ident_bf[:], nomemset=True)
         make_identity(nc, ident_f32[:])
         nc.scalar.dma_start(out=c_rows[0:TILES, :], in_=c_slow.rearrange("(a p) -> a p", p=P))
         nc.scalar.dma_start(out=c_rows[TILES : 2 * TILES, :], in_=c_mid.rearrange("(a p) -> a p", p=P))
-        load_scales(nc.scalar, xs, x_scales)
+        load_scales(nc.scalar, xs[0], x_scales[:, :, 0:GROUP])
         load_w(0)
         load_x(0, 0)
         load_scales(nc.sync, fs, fast_scales)
         nc.sync.dma_start(out=fw[:].bitcast(I32), in_=fast_words.rearrange("g p n -> p g n").bitcast(I32))
         load_x(0, 1)
-        load_w(1)
         load_x(0, 2)
+        load_w(1)
         load_w(2)
         load_scales(nc.sync, ms, mid_scales)
-        nc.sync.dma_start(out=mw[:], in_=mid_words.rearrange("g p n t -> p g (n t)").bitcast(I32))
+        load_m(0, 2)
+        load_scales(nc.sync, xs[1], x_scales[:, :, GROUP:J])
+        load_m(2, 2)
         for g in range(PASSES):
             load_x(1, g)
 
@@ -182,101 +216,110 @@ def tile_windowed_resolvent_response_k3_kernel(
                 lhsT=ident_bf[:, row : row + 1].to_broadcast([P, P]), rhs=c_rows[:], start=True, stop=True,
             )
 
+        for w in range(BRIDGE):
+            nc.tensor.matmul(bank[4][:], lhsT=warm[:, 0:P], rhs=w_raw[0][:, w, :], start=True, stop=True)
+        nc.vector.tensor_copy(out=c_cols[:], in_=bank[5][:, 0 : 2 * TILES])
         group_w(nc.vector.tensor_copy, 0, 0, 1)
         group_w(nc.scalar.copy, 0, 1, 1)
+        quant_w(0, 0, 1)
         group_w(nc.vector.tensor_copy, 0, 2, 1)
         group_w(nc.scalar.copy, 0, 3, 1)
-        quant_w(0, 0, 1)
-        quant_w(0, 1, 1)
-        quant_w(0, 2, 1)
-        nc.vector.tensor_copy(out=c_cols[:], in_=bank[5][:, 0 : 2 * TILES])
-        quant_w(0, 3, 1)
         nc.scalar.copy(out=cs_wide[:], in_=bank[6][:])
         nc.scalar.copy(out=cm_wide[:], in_=bank[7][:])
-
-        for a in range(TILES):
-            pass_sensors("slow", 0, a, a)
-        for g in (0, 1):
-            for a in range(TILES):
-                pass_sensors("fast", g, a, 4 + a)
+        quant_w(0, 1, 1)
+        quant_w(0, 2, 1)
+        quant_w(0, 3, 1)
         for g in (1, 2):
-            group_w(nc.vector.tensor_copy, g, 0, 2)
-            group_w(nc.scalar.copy, g, 2, 2)
-            quant_w(g, 0, 2)
-            quant_w(g, 2, 2)
+            group_w(nc.vector.tensor_copy, g, 0, 1)
+            group_w(nc.scalar.copy, g, 1, 1)
+            group_w(nc.vector.tensor_copy, g, 2, 1)
+            group_w(nc.scalar.copy, g, 3, 1)
+            for a in range(TILES):
+                quant_w(g, a, 1)
+
+        for kind, g in (("slow", 0), ("fast", 0), ("fast", 1), ("fast", 2), ("slow", 1), ("slow", 2)):
+            for a in range(TILES):
+                pass_sensors(kind, g, a, a if kind == "slow" else 4 + a)
         for a in range(TILES):
-            pass_sensors("slow", 1, a, a)
-        for a in range(TILES):
-            pass_sensors("fast", 2, a, 4 + a)
             nc.scalar.copy(out=f_t[a][:], in_=sorted_bank(4 + a))
-        for a in range(TILES):
-            pass_sensors("slow", 2, a, a)
-            nc.vector.scalar_tensor_tensor(
-                out=p_t[a][:], in0=sorted_bank(a), scalar=c_cols[:, a : a + 1], in1=f_t[a][:], op0=MULT, op1=ADD
-            )
+            combine(p_t[a], a, a, f_t[a])
         for a in range(TILES):
             for g in range(PASSES):
                 pass_sensors("mid", g, a, 4 + a)
-            if a < PASSES:
-                sort_x(a)
-            nc.vector.scalar_tensor_tensor(
-                out=y_t[a][:], in0=sorted_bank(4 + a), scalar=c_cols[:, TILES + a : TILES + a + 1], in1=p_t[a][:],
-                op0=MULT, op1=ADD,
-            )
+        for g in range(PASSES):
+            sort_x(g)
 
-        def leave_turned(a, b):
-            nc.scalar.copy(
-                out=y16[0][a][:].rearrange("p (i t) -> p i t", t=PACK),
-                in_=bank[b][:].rearrange("p (t i) -> p i t", t=PACK),
-            )
-            nc.scalar.copy(out=y32[0][a][:], in_=bank[b][:].rearrange("p (t i) -> p t i", t=PACK))
-            store_y(0, a)
-
-        def mid_and_slow(t, b):
+        def product(kind, t, b):
             for g in range(PASSES):
-                pass_modes("mid", g, t, bank[b][:], 0, TILES)
+                pass_modes(kind, g, t, bank[b][:], 0, TILES)
+
+        def scale_mid(t, b):
             nc.vector.tensor_tensor(out=m_n[t][:], in0=bank[b][:], in1=cm_wide[:], op=MULT)
-            for g in range(PASSES):
-                pass_modes("slow", g, t, bank[b + 1][:], 0, TILES)
-            nc.vector.tensor_tensor(out=s_n[t][:], in0=bank[b + 1][:], in1=cs_wide[:], op=MULT)
+
+        def scale_slow(t, b):
+            nc.vector.tensor_tensor(out=s_n[t][:], in0=bank[b][:], in1=cs_wide[:], op=MULT)
             adder = nc.vector if t == PACK - 1 else nc.gpsimd
             adder.tensor_tensor(out=q_n[:, t, :], in0=m_n[t][:], in1=s_n[t][:], op=ADD)
 
-        for a in (0, 1):
-            turn(a, a)
-            leave_turned(a, a)
-        mid_and_slow(0, 2)
-        quant_y(0, 0)
-        for a in (2, 3):
-            turn(a, 2 + a)
-            leave_turned(a, 2 + a)
-        mid_and_slow(1, 6)
-        quant_y(0, 1)
-        quant_y(0, 2)
-        mid_and_slow(2, 0)
-        quant_y(0, 3)
-        store_words(0, 0, TILES)
-        mid_and_slow(3, 2)
+        def finish(a, b):
+            turn(a, b)
+            leave_turned(0, a, b)
 
-        for a in range(TILES):
-            for t in range(PACK):
-                for g in range(PASSES):
-                    pass_modes("fast", g, t, bank[4 + a][:, cols(t)], a, 1)
-            nc.vector.tensor_tensor(
-                out=y32[1][a][:], in0=bank[4 + a][:].rearrange("p (t i) -> p t i", t=PACK), in1=q_n[:, :, cols(a)], op=ADD
-            )
-            store_y(1, a)
-            nc.scalar.copy(
+        def store_rows(t, nt, a, n):
+            rows = out_0[GROUP:J, :].rearrange("(p t) m -> p t m", t=PACK)
+            nc.sync.dma_start(out=rows[:, t : t + nt, cols(a, n)], in_=y_n[:, t : t + nt, cols(a, n)])
+
+        def group_y(copy, a):
+            copy(
                 out=y16[1][a][:].rearrange("p (c i t) -> p c t i", i=4, t=PACK),
-                in_=y32[1][a][:].rearrange("p t (c i) -> p c t i", i=4),
+                in_=y_n[:, :, cols(a)].rearrange("p t (c i) -> p c t i", i=4),
             )
-            if a > 0:
-                quant_y(1, a - 1)
-                store_words(1, a - 1, 1)
-        quant_y(1, TILES - 1)
-        store_words(1, TILES - 1, 1)
-        for r in range(4):
-            eng = nc.scalar if r % 2 else nc.sync
-            eng.dma_start(
-                out=out_2[:, r:16:4, :].rearrange("g q n -> q g n").bitcast(I32), in_=ysc[r:P:32, :, :].bitcast(I32)
+
+        product("mid", 0, 0)
+        product("slow", 0, 1)
+        for a in (0, 1):
+            combine(y_t[a], 4 + a, TILES + a, p_t[a])
+            finish(a, 2 + a)
+        scale_mid(0, 0)
+        product("mid", 1, 4)
+        product("slow", 1, 5)
+        combine(y_t[2], 6, TILES + 2, p_t[2])
+        scale_slow(0, 1)
+        combine(y_t[3], 7, TILES + 3, p_t[3])
+        for a in (2, 3):
+            finish(a, 4 + a)
+        scale_mid(1, 4)
+        scale_slow(1, 5)
+        for t in (2, 3):
+            quant_y(0, 2 * t - 4)
+            quant_y(0, 2 * t - 3)
+            product("mid", t, 2 * t - 4)
+            scale_mid(t, 2 * t - 4)
+            product("slow", t, 2 * t - 3)
+            scale_slow(t, 2 * t - 3)
+        store_words(0, 0, TILES)
+        for t in (0, 1):
+            product("fast", t, 4 + t)
+            nc.vector.tensor_tensor(out=y_n[:, t, :], in0=bank[4 + t][:], in1=q_n[:, t, :], op=ADD)
+            store_rows(t, 1, 0, TILES)
+        for a in range(TILES):
+            b = (6 + a) % 8
+            for t in (2, 3):
+                for g in range(PASSES):
+                    pass_modes("fast", g, t, bank[b][:, cols(t - 2)], a, 1)
+            nc.vector.tensor_tensor(
+                out=y_n[:, 2:4, cols(a)], in0=bank[b][:, 0 : 2 * P].rearrange("p (t i) -> p t i", t=2),
+                in1=q_n[:, 2:4, cols(a)], op=ADD,
             )
+            if a % 2:
+                store_rows(2, 2, a - 1, 2)
+            if a < TILES - 1:
+                group_y(nc.scalar.copy, a)
+        quant_y(1, 0)
+        group_y(nc.vector.tensor_copy, TILES - 1)
+        quant_y(1, 1)
+        store_words(1, 0, 2)
+        quant_y(1, 3)
+        quant_y(1, 2)
+        store_words(1, 2, 2)
+        store_scales()

@@ -64,8 +64,8 @@ def tile_windowed_resolvent_response_k3_kernel(
         s_n = [sbuf("s_n%d" % t, [P, N], F32) for t in range(PACK)]
         q_n = sbuf("q_n", [P, PACK, N], F32)
         y_n = sbuf("y_n", [P, PACK, N], F32)
-        y32 = [[sbuf("y32_%d_%d" % (h, a), [P, PACK, P], F32) for a in range(TILES)] for h in range(2)]
-        y16 = [[sbuf("y16_%d_%d" % (h, a), [P, P * PACK], BF16) for a in range(TILES)] for h in range(2)]
+        y32 = [sbuf("y32_%d" % u, [P, PACK, 2 * P], F32) for u in range(2)]
+        y16 = [sbuf("y16_%d" % h, [P, N * PACK], BF16) for h in range(2)]
         yq = [sbuf("yq%d" % h, [P, N], I32) for h in range(2)]
         ysc = sbuf("ysc", [P, 2, N], U8)
 
@@ -125,11 +125,13 @@ def tile_windowed_resolvent_response_k3_kernel(
         def sorted_bank(b):
             return bank[b][:].rearrange("i (m t) -> i t m", t=PACK)
 
-        def sort_x(g):
+        def sort_x_words(g):
             nc.vector.tensor_copy(
                 out=xp[g][:].rearrange("p t (c i) -> p c t i", i=4),
                 in_=xw[1][g][:].rearrange("p (c i t) -> p c t i", i=4, t=PACK),
             )
+
+        def sort_x_scales(g):
             nc.vector.tensor_copy(
                 out=xps[g][:].rearrange("p t (c i) -> p c t i", i=16),
                 in_=xs[1][:, g, :].rearrange("p (c i t) -> p c t i", i=16, t=PACK),
@@ -139,22 +141,20 @@ def tile_windowed_resolvent_response_k3_kernel(
             for t in range(PACK):
                 nc.tensor.transpose(bank[b][:, cols(t)], y_t[a][:, t, :], ident_f32[:])
 
-        def quant_y(h, a):
+        def quant_y(h, a, n=1):
             nc.vector.quantize_mx(
-                out=yq[h][:, cols(a)].bitcast(FP8X4), scales=ysc[:, h, cols(a)], in_=y16[h][a][:]
+                out=yq[h][:, cols(a, n)].bitcast(FP8X4), scales=ysc[:, h, cols(a, n)],
+                in_=y16[h][:, a * GROUP : (a + n) * GROUP],
             )
 
-        def store_y(h, a):
-            rows = out_0[h * GROUP : (h + 1) * GROUP, cols(a)]
-            nc.sync.dma_start(out=rows.rearrange("(p t) m -> p t m", t=PACK), in_=y32[h][a][:])
+        def store_y(u):
+            rows = out_0[0:GROUP, cols(2 * u, 2)]
+            nc.sync.dma_start(out=rows.rearrange("(p t) m -> p t m", t=PACK), in_=y32[u][:])
 
         def store_words(h, a, n):
             dst = out_1[h].rearrange("p n t -> p (n t)").bitcast(I32)
             nc.sync.dma_start(out=dst[:, cols(a, n)], in_=yq[h][:, cols(a, n)])
 
-
-        def load_f(g):
-            nc.sync.dma_start(out=fw[g][:].bitcast(I32), in_=fast_words[g].bitcast(I32))
 
         def load_m(a, n):
             src = mid_words.rearrange("g p n t -> p g (n t)").bitcast(I32)
@@ -165,20 +165,18 @@ def tile_windowed_resolvent_response_k3_kernel(
                 out=out[:], in0=sorted_bank(b), scalar=c_cols[:, col : col + 1], in1=other[:], op0=MULT, op1=ADD
             )
 
-        def leave_turned(h, a, b):
-            nc.scalar.copy(out=y32[h][a][:], in_=bank[b][:].rearrange("p (t i) -> p t i", t=PACK))
-            store_y(h, a)
-            nc.scalar.copy(
-                out=y16[h][a][:].rearrange("p (i t) -> p i t", t=PACK),
-                in_=bank[b][:].rearrange("p (t i) -> p i t", t=PACK),
-            )
-
-        def store_scales():
-            for r in range(4):
-                eng = nc.scalar if r % 2 else nc.sync
-                eng.dma_start(
-                    out=out_2[:, r:16:4, :].rearrange("g q n -> q g n").bitcast(I32), in_=ysc[r:P:32, :, :].bitcast(I32)
+        def leave_turned(u, b):
+            for a in (0, 1):
+                nc.scalar.copy(
+                    out=y16[0][:, (2 * u + a) * GROUP : (2 * u + a + 1) * GROUP].rearrange("p (i t) -> p i t", t=PACK),
+                    in_=bank[b + a][:].rearrange("p (t i) -> p i t", t=PACK),
                 )
+                nc.scalar.copy(out=y32[u][:, :, cols(a)], in_=bank[b + a][:].rearrange("p (t i) -> p t i", t=PACK))
+            store_y(u)
+
+        def store_scales(h, engines):
+            for r in range(4):
+                engines[r % 2].dma_start(out=out_2[h, r:16:4, :].bitcast(I32), in_=ysc[r:P:32, h, :].bitcast(I32))
 
         nc.vector.memset(c_rows[:], 0.0)
         nc.vector.memset(xs[0][:].bitcast(I32), 0)
@@ -201,9 +199,8 @@ def tile_windowed_resolvent_response_k3_kernel(
         load_w(1)
         load_w(2)
         load_scales(nc.sync, ms, mid_scales)
-        load_m(0, 2)
+        load_m(0, 4)
         load_scales(nc.sync, xs[1], x_scales[:, :, GROUP:J])
-        load_m(2, 2)
         for g in range(PASSES):
             load_x(1, g)
 
@@ -229,13 +226,22 @@ def tile_windowed_resolvent_response_k3_kernel(
         quant_w(0, 1, 1)
         quant_w(0, 2, 1)
         quant_w(0, 3, 1)
-        for g in (1, 2):
-            group_w(nc.vector.tensor_copy, g, 0, 1)
-            group_w(nc.scalar.copy, g, 1, 1)
-            group_w(nc.vector.tensor_copy, g, 2, 1)
-            group_w(nc.scalar.copy, g, 3, 1)
-            for a in range(TILES):
-                quant_w(g, a, 1)
+        group_w(nc.scalar.copy, 1, 3, 1)
+        group_w(nc.vector.tensor_copy, 1, 0, 1)
+        group_w(nc.vector.tensor_copy, 1, 1, 1)
+        quant_w(1, 0, 1)
+        group_w(nc.vector.tensor_copy, 1, 2, 1)
+        quant_w(1, 1, 1)
+        quant_w(1, 2, 1)
+        quant_w(1, 3, 1)
+        group_w(nc.scalar.copy, 2, 0, 1)
+        group_w(nc.scalar.copy, 2, 2, 1)
+        group_w(nc.vector.tensor_copy, 2, 1, 1)
+        quant_w(2, 0, 1)
+        quant_w(2, 1, 1)
+        group_w(nc.vector.tensor_copy, 2, 3, 1)
+        quant_w(2, 2, 1)
+        quant_w(2, 3, 1)
 
         for kind, g in (("slow", 0), ("fast", 0), ("fast", 1), ("fast", 2), ("slow", 1), ("slow", 2)):
             for a in range(TILES):
@@ -247,7 +253,8 @@ def tile_windowed_resolvent_response_k3_kernel(
             for g in range(PASSES):
                 pass_sensors("mid", g, a, 4 + a)
         for g in range(PASSES):
-            sort_x(g)
+            sort_x_words(g)
+            sort_x_scales(g)
 
         def product(kind, t, b):
             for g in range(PASSES):
@@ -258,12 +265,8 @@ def tile_windowed_resolvent_response_k3_kernel(
 
         def scale_slow(t, b):
             nc.vector.tensor_tensor(out=s_n[t][:], in0=bank[b][:], in1=cs_wide[:], op=MULT)
-            adder = nc.vector if t == PACK - 1 else nc.gpsimd
-            adder.tensor_tensor(out=q_n[:, t, :], in0=m_n[t][:], in1=s_n[t][:], op=ADD)
-
-        def finish(a, b):
-            turn(a, b)
-            leave_turned(0, a, b)
+            for half in (cols(0, 2), cols(2, 2)):
+                nc.gpsimd.tensor_tensor(out=q_n[:, t, half], in0=m_n[t][:, half], in1=s_n[t][:, half], op=ADD)
 
         def store_rows(t, nt, a, n):
             rows = out_0[GROUP:J, :].rearrange("(p t) m -> p t m", t=PACK)
@@ -271,7 +274,7 @@ def tile_windowed_resolvent_response_k3_kernel(
 
         def group_y(copy, a):
             copy(
-                out=y16[1][a][:].rearrange("p (c i t) -> p c t i", i=4, t=PACK),
+                out=y16[1][:, a * GROUP : (a + 1) * GROUP].rearrange("p (c i t) -> p c t i", i=4, t=PACK),
                 in_=y_n[:, :, cols(a)].rearrange("p t (c i) -> p c t i", i=4),
             )
 
@@ -279,7 +282,8 @@ def tile_windowed_resolvent_response_k3_kernel(
         product("slow", 0, 1)
         for a in (0, 1):
             combine(y_t[a], 4 + a, TILES + a, p_t[a])
-            finish(a, 2 + a)
+            turn(a, 2 + a)
+        leave_turned(0, 2)
         scale_mid(0, 0)
         product("mid", 1, 4)
         product("slow", 1, 5)
@@ -287,17 +291,19 @@ def tile_windowed_resolvent_response_k3_kernel(
         scale_slow(0, 1)
         combine(y_t[3], 7, TILES + 3, p_t[3])
         for a in (2, 3):
-            finish(a, 4 + a)
+            turn(a, 4 + a)
+        leave_turned(1, 6)
         scale_mid(1, 4)
         scale_slow(1, 5)
         for t in (2, 3):
-            quant_y(0, 2 * t - 4)
-            quant_y(0, 2 * t - 3)
             product("mid", t, 2 * t - 4)
             scale_mid(t, 2 * t - 4)
+            if t == 2:
+                quant_y(0, 0, TILES)
+                store_words(0, 0, TILES)
+                store_scales(0, (nc.sync, nc.sync))
             product("slow", t, 2 * t - 3)
             scale_slow(t, 2 * t - 3)
-        store_words(0, 0, TILES)
         for t in (0, 1):
             product("fast", t, 4 + t)
             nc.vector.tensor_tensor(out=y_n[:, t, :], in0=bank[4 + t][:], in1=q_n[:, t, :], op=ADD)
@@ -322,4 +328,4 @@ def tile_windowed_resolvent_response_k3_kernel(
         quant_y(1, 3)
         quant_y(1, 2)
         store_words(1, 2, 2)
-        store_scales()
+        store_scales(1, (nc.scalar, nc.sync))

from contextlib import ExitStack

import concourse.mybir as mybir
from concourse.masks import make_identity

J, K, N = 1024, 1536, 512
FLOPS = 3 * 2 * J * K * N

F32 = mybir.dt.float32
BF16 = mybir.dt.bfloat16
I32 = mybir.dt.int32
U8 = mybir.dt.uint8
FP8X4 = mybir.dt.float8_e4m3fn_x4
FP4X4 = mybir.dt.float4_e2m1fn_x4
MULT = mybir.AluOpType.mult
ADD = mybir.AluOpType.add

P = 128
PACK = 4
GROUP = P * PACK
PASSES = K // GROUP
TILES = N // P
WARM = 3
BRIDGE = 3


def tile_windowed_resolvent_response_k3_kernel(
    tc, x_words, x_scales, w_slow, mid_words, mid_scales, fast_words, fast_scales, c_slow, c_mid, out_0, out_1, out_2
):
    nc = tc.nc
    with ExitStack() as ctx:
        sb = ctx.enter_context(tc.tile_pool(name="sb", bufs=1))
        ps = ctx.enter_context(tc.psum_pool(name="ps", bufs=1))
        ctx.enter_context(tc.manual_schedule())

        def sbuf(name, shape, dtype):
            return sb.tile(shape, dtype, name=name, align_bytes=64)

        bank = [ps.tile([P, N], F32, name="bank%d" % b) for b in range(8)]

        c_rows = sbuf("c_rows", [P, P], BF16)
        ident_bf = sbuf("ident_bf", [P, P], BF16)
        ident_f32 = sbuf("ident_f32", [P, P], F32)
        warm = sbuf("warm", [P, N], BF16)
        c_cols = sbuf("c_cols", [P, 2 * TILES], F32)
        cs_wide = sbuf("cs_wide", [P, N], F32)
        cm_wide = sbuf("cm_wide", [P, N], F32)
        xs = [sbuf("xs%d" % h, [P, PASSES, GROUP], U8) for h in range(2)]
        fs = sbuf("fs", [P, PASSES, N], U8)
        ms = sbuf("ms", [P, PASSES, N], U8)
        xw = [[sbuf("xw%d_%d" % (h, g), [P, GROUP], I32) for g in range(PASSES)] for h in range(2)]
        xp = [sbuf("xp%d" % g, [P, PACK, P], I32) for g in range(PASSES)]
        xps = [sbuf("xps%d" % g, [P, PACK, P], U8) for g in range(PASSES)]
        fw = sbuf("fw", [P, PASSES, 2 * N], U8)
        mw = sbuf("mw", [P, PASSES, N], I32)
        w_raw = [sbuf("w_raw%d" % g, [P, PACK, N], BF16) for g in range(PASSES)]
        w_grp = [sbuf("w_grp%d" % g, [P, N * PACK], BF16) for g in range(PASSES)]
        sw = [sbuf("sw%d" % g, [P, N], I32) for g in range(PASSES)]
        ss = [sbuf("ss%d" % g, [P, N], U8) for g in range(PASSES)]
        f_t = [sbuf("f_t%d" % a, [P, PACK, P], F32) for a in range(TILES)]
        p_t = [sbuf("p_t%d" % a, [P, PACK, P], F32) for a in range(TILES)]
        y_t = [sbuf("y_t%d" % a, [P, PACK, P], F32) for a in range(TILES)]
        m_n = [sbuf("m_n%d" % t, [P, N], F32) for t in range(PACK)]
        s_n = [sbuf("s_n%d" % t, [P, N], F32) for t in range(PACK)]
        q_n = sbuf("q_n", [P, PACK, N], F32)
        y_n = sbuf("y_n", [P, PACK, N], F32)
        y32 = [sbuf("y32_%d" % u, [P, PACK, 2 * P], F32) for u in range(2)]
        y16 = [sbuf("y16_%d" % h, [P, N * PACK], BF16) for h in range(2)]
        yq = [sbuf("yq%d" % h, [P, N], I32) for h in range(2)]
        ysc = sbuf("ysc", [P, 2, N], U8)

        def cols(a, n=1):
            return slice(a * P, (a + n) * P)

        def load_scales(eng, plane, src):
            for r in range(4):
                eng.dma_start(
                    out=plane[r:P:32, :, :].bitcast(I32),
                    in_=src[:, r:16:4, :].rearrange("g q n -> q g n").bitcast(I32),
                )

        def load_x(h, g):
            src = x_words[g].rearrange("p n t -> p (n t)").bitcast(I32)
            nc.sync.dma_start(out=xw[h][g][:], in_=src[:, h * GROUP : (h + 1) * GROUP])

        def load_w(g):
            nc.sync.dma_start(
                out=w_raw[g][:], in_=w_slow[g * GROUP : (g + 1) * GROUP, :].rearrange("(p t) n -> p t n", t=PACK)
            )

        def group_w(copy, g, a, n):
            copy(
                out=w_grp[g][:, a * GROUP : (a + n) * GROUP].rearrange("p (c i t) -> p c t i", i=4, t=PACK),
                in_=w_raw[g][:, :, cols(a, n)].rearrange("p t (c i) -> p c t i", i=4),
            )

        def quant_w(g, a, n):
            nc.vector.quantize_mx(
                out=sw[g][:, cols(a, n)].bitcast(FP8X4),
                scales=ss[g][:, cols(a, n)],
                in_=w_grp[g][:, a * GROUP : (a + n) * GROUP],
            )

        def weight(kind, g, a, n):
            if kind == "slow":
                return sw[g][:, cols(a, n)].bitcast(FP8X4), ss[g][:, cols(a, n)]
            if kind == "mid":
                return mw[:, g, cols(a, n)].bitcast(FP8X4), ms[:, g, cols(a, n)]
            return fw[:, g, 2 * a * P : 2 * (a + n) * P].bitcast(FP4X4), fs[:, g, cols(a, n)]

        def pass_sensors(kind, g, a, b, h=0):
            w, s = weight(kind, g, a, 1)
            nc.tensor.matmul_mx(
                out=bank[b][:], lhsT=w, lhsT_scale=s, rhs=xw[h][g][:].bitcast(FP8X4), rhs_scale=xs[h][:, g, :],
                start=(g == 0), stop=(g == PASSES - 1),
            )

        def pass_modes(kind, g, t, out, a, n):
            w, s = weight(kind, g, a, n)
            nc.tensor.matmul_mx(
                out=out, lhsT=xp[g][:, t, :].bitcast(FP8X4), lhsT_scale=xps[g][:, t, :], rhs=w, rhs_scale=s,
                start=(g == 0), stop=(g == PASSES - 1),
            )

        def sorted_bank(b):
            return bank[b][:].rearrange("i (m t) -> i t m", t=PACK)

        def sort_x_words(g):
            nc.vector.tensor_copy(
                out=xp[g][:].rearrange("p t (c i) -> p c t i", i=4),
                in_=xw[1][g][:].rearrange("p (c i t) -> p c t i", i=4, t=PACK),
            )

        def sort_x_scales(g):
            nc.vector.tensor_copy(
                out=xps[g][:].rearrange("p t (c i) -> p c t i", i=16),
                in_=xs[1][:, g, :].rearrange("p (c i t) -> p c t i", i=16, t=PACK),
            )

        def turn(a, b):
            for t in range(PACK):
                nc.tensor.transpose(bank[b][:, cols(t)], y_t[a][:, t, :], ident_f32[:])

        def quant_y(h, a, n=1):
            nc.vector.quantize_mx(
                out=yq[h][:, cols(a, n)].bitcast(FP8X4), scales=ysc[:, h, cols(a, n)],
                in_=y16[h][:, a * GROUP : (a + n) * GROUP],
            )

        def store_y(u):
            rows = out_0[0:GROUP, cols(2 * u, 2)]
            nc.sync.dma_start(out=rows.rearrange("(p t) m -> p t m", t=PACK), in_=y32[u][:])

        def store_words(h, a, n):
            dst = out_1[h].rearrange("p n t -> p (n t)").bitcast(I32)
            nc.sync.dma_start(out=dst[:, cols(a, n)], in_=yq[h][:, cols(a, n)])


        def load_m(a, n):
            src = mid_words.rearrange("g p n t -> p g (n t)").bitcast(I32)
            nc.sync.dma_start(out=mw[:, :, cols(a, n)], in_=src[:, :, cols(a, n)])

        def combine(out, b, col, other):
            nc.vector.scalar_tensor_tensor(
                out=out[:], in0=sorted_bank(b), scalar=c_cols[:, col : col + 1], in1=other[:], op0=MULT, op1=ADD
            )

        def leave_turned(u, b):
            for a in (0, 1):
                nc.scalar.copy(
                    out=y16[0][:, (2 * u + a) * GROUP : (2 * u + a + 1) * GROUP].rearrange("p (i t) -> p i t", t=PACK),
                    in_=bank[b + a][:].rearrange("p (t i) -> p i t", t=PACK),
                )
                nc.scalar.copy(out=y32[u][:, :, cols(a)], in_=bank[b + a][:].rearrange("p (t i) -> p t i", t=PACK))
            store_y(u)

        def store_scales(h, engines):
            for r in range(4):
                engines[r % 2].dma_start(out=out_2[h, r:16:4, :].bitcast(I32), in_=ysc[r:P:32, h, :].bitcast(I32))

        nc.vector.memset(c_rows[:], 0.0)
        nc.vector.memset(xs[0][:].bitcast(I32), 0)
        nc.vector.memset(ident_bf[:], 0.0)
        nc.vector.memset(fs[:].bitcast(I32), 0)
        nc.vector.memset(ms[:].bitcast(I32), 0)
        nc.vector.memset(xs[1][:].bitcast(I32), 0)
        nc.gpsimd.memset(warm[:], 0.0)
        make_identity(nc, ident_bf[:], nomemset=True)
        make_identity(nc, ident_f32[:])
        nc.scalar.dma_start(out=c_rows[0:TILES, :], in_=c_slow.rearrange("(a p) -> a p", p=P))
        nc.scalar.dma_start(out=c_rows[TILES : 2 * TILES, :], in_=c_mid.rearrange("(a p) -> a p", p=P))
        load_scales(nc.scalar, xs[0], x_scales[:, :, 0:GROUP])
        load_w(0)
        load_x(0, 0)
        load_scales(nc.sync, fs, fast_scales)
        nc.sync.dma_start(out=fw[:].bitcast(I32), in_=fast_words.rearrange("g p n -> p g n").bitcast(I32))
        load_x(0, 1)
        load_x(0, 2)
        load_w(1)
        load_w(2)
        load_scales(nc.sync, ms, mid_scales)
        load_m(0, 4)
        load_scales(nc.sync, xs[1], x_scales[:, :, GROUP:J])
        for g in range(PASSES):
            load_x(1, g)

        for w in range(WARM):
            nc.tensor.matmul(bank[4][:], lhsT=warm[:, 0:P], rhs=warm[:], start=True, stop=True)
        nc.tensor.matmul(bank[5][:, 0 : 2 * TILES], lhsT=c_rows[:], rhs=ident_bf[:, 0 : 2 * TILES], start=True, stop=True)
        for row in range(2 * TILES):
            nc.tensor.matmul(
                bank[6 + row // TILES][:, cols(row % TILES)],
                lhsT=ident_bf[:, row : row + 1].to_broadcast([P, P]), rhs=c_rows[:], start=True, stop=True,
            )

        for w in range(BRIDGE):
            nc.tensor.matmul(bank[4][:], lhsT=warm[:, 0:P], rhs=w_raw[0][:, w, :], start=True, stop=True)
        nc.vector.tensor_copy(out=c_cols[:], in_=bank[5][:, 0 : 2 * TILES])
        group_w(nc.vector.tensor_copy, 0, 0, 1)
        group_w(nc.scalar.copy, 0, 1, 1)
        quant_w(0, 0, 1)
        group_w(nc.vector.tensor_copy, 0, 2, 1)
        group_w(nc.scalar.copy, 0, 3, 1)
        nc.scalar.copy(out=cs_wide[:], in_=bank[6][:])
        nc.scalar.copy(out=cm_wide[:], in_=bank[7][:])
        quant_w(0, 1, 1)
        quant_w(0, 2, 1)
        quant_w(0, 3, 1)
        group_w(nc.scalar.copy, 1, 3, 1)
        group_w(nc.vector.tensor_copy, 1, 0, 1)
        group_w(nc.vector.tensor_copy, 1, 1, 1)
        quant_w(1, 0, 1)
        group_w(nc.vector.tensor_copy, 1, 2, 1)
        quant_w(1, 1, 1)
        quant_w(1, 2, 1)
        quant_w(1, 3, 1)
        group_w(nc.scalar.copy, 2, 0, 1)
        group_w(nc.scalar.copy, 2, 2, 1)
        group_w(nc.vector.tensor_copy, 2, 1, 1)
        quant_w(2, 0, 1)
        quant_w(2, 1, 1)
        group_w(nc.vector.tensor_copy, 2, 3, 1)
        quant_w(2, 2, 1)
        quant_w(2, 3, 1)

        for kind, g in (("slow", 0), ("fast", 0), ("fast", 1), ("fast", 2), ("slow", 1), ("slow", 2)):
            for a in range(TILES):
                pass_sensors(kind, g, a, a if kind == "slow" else 4 + a)
        for a in range(TILES):
            nc.scalar.copy(out=f_t[a][:], in_=sorted_bank(4 + a))
            combine(p_t[a], a, a, f_t[a])
        for a in range(TILES):
            for g in range(PASSES):
                pass_sensors("mid", g, a, 4 + a)
        for g in range(PASSES):
            sort_x_words(g)
            sort_x_scales(g)

        def product(kind, t, b):
            for g in range(PASSES):
                pass_modes(kind, g, t, bank[b][:], 0, TILES)

        def scale_mid(t, b):
            nc.vector.tensor_tensor(out=m_n[t][:], in0=bank[b][:], in1=cm_wide[:], op=MULT)

        def scale_slow(t, b):
            nc.vector.tensor_tensor(out=s_n[t][:], in0=bank[b][:], in1=cs_wide[:], op=MULT)
            for half in (cols(0, 2), cols(2, 2)):
                nc.gpsimd.tensor_tensor(out=q_n[:, t, half], in0=m_n[t][:, half], in1=s_n[t][:, half], op=ADD)

        def store_rows(t, nt, a, n):
            rows = out_0[GROUP:J, :].rearrange("(p t) m -> p t m", t=PACK)
            nc.sync.dma_start(out=rows[:, t : t + nt, cols(a, n)], in_=y_n[:, t : t + nt, cols(a, n)])

        def group_y(copy, a):
            copy(
                out=y16[1][:, a * GROUP : (a + 1) * GROUP].rearrange("p (c i t) -> p c t i", i=4, t=PACK),
                in_=y_n[:, :, cols(a)].rearrange("p t (c i) -> p c t i", i=4),
            )

        product("mid", 0, 0)
        product("slow", 0, 1)
        for a in (0, 1):
            combine(y_t[a], 4 + a, TILES + a, p_t[a])
            turn(a, 2 + a)
        leave_turned(0, 2)
        scale_mid(0, 0)
        product("mid", 1, 4)
        product("slow", 1, 5)
        combine(y_t[2], 6, TILES + 2, p_t[2])
        scale_slow(0, 1)
        combine(y_t[3], 7, TILES + 3, p_t[3])
        for a in (2, 3):
            turn(a, 4 + a)
        leave_turned(1, 6)
        scale_mid(1, 4)
        scale_slow(1, 5)
        for t in (2, 3):
            product("mid", t, 2 * t - 4)
            scale_mid(t, 2 * t - 4)
            if t == 2:
                quant_y(0, 0, TILES)
                store_words(0, 0, TILES)
                store_scales(0, (nc.sync, nc.sync))
            product("slow", t, 2 * t - 3)
            scale_slow(t, 2 * t - 3)
        for t in (0, 1):
            product("fast", t, 4 + t)
            nc.vector.tensor_tensor(out=y_n[:, t, :], in0=bank[4 + t][:], in1=q_n[:, t, :], op=ADD)
            store_rows(t, 1, 0, TILES)
        for a in range(TILES):
            b = (6 + a) % 8
            for t in (2, 3):
                for g in range(PASSES):
                    pass_modes("fast", g, t, bank[b][:, cols(t - 2)], a, 1)
            nc.vector.tensor_tensor(
                out=y_n[:, 2:4, cols(a)], in0=bank[b][:, 0 : 2 * P].rearrange("p (t i) -> p t i", t=2),
                in1=q_n[:, 2:4, cols(a)], op=ADD,
            )
            if a % 2:
                store_rows(2, 2, a - 1, 2)
            if a < TILES - 1:
                group_y(nc.scalar.copy, a)
        quant_y(1, 0)
        group_y(nc.vector.tensor_copy, TILES - 1)
        quant_y(1, 1)
        store_words(1, 0, 2)
        quant_y(1, 3)
        quant_y(1, 2)
        store_words(1, 2, 2)
        store_scales(1, (nc.scalar, nc.sync))
